import numpy as np
import ml_dtypes


def mxq(x, axis, fmt="e4m3"):
    dtype, down = {"e4m3": (ml_dtypes.float8_e4m3fn, 7), "e5m2": (ml_dtypes.float8_e5m2, 14)}[fmt]
    v = np.moveaxis(np.asarray(x, np.float32).astype(ml_dtypes.bfloat16).astype(np.float64), axis, -1)
    blocks = v.reshape(v.shape[:-1] + (-1, 32))
    amax = np.abs(blocks).max(-1, keepdims=True)
    byte = np.maximum(np.where(amax > 0, np.frexp(amax)[1] - 1 + 127, 0) - down, 1)
    scale = np.exp2(byte - 127.0)
    codes = (blocks / scale).astype(np.float32).astype(dtype).astype(np.float64)
    return np.moveaxis((codes * scale).reshape(v.shape), -1, axis)


WIDE = False


def mx_kscale(k):
    if not WIDE:
        return np.ones(k)
    levels = np.array([10, -10, 5, -5, 0])
    if k % 512:
        return np.exp2(np.random.permutation(np.resize(levels, k // 32))).repeat(32)
    a = np.empty((k // 512, 16))
    for p in range(k // 512):
        a[p, :8] = np.random.permutation(np.resize(levels, 8))
        for g in range(8):
            far = levels[np.abs(levels - a[p, g]) >= 10]
            a[p, g + 8] = far[np.random.randint(len(far))]
    return np.exp2(a.ravel()).repeat(32)


def f64(x):
    return np.asarray(x).astype(np.float64)


def striped(idx):
    return np.tile(np.asarray(idx).reshape(-1, 16).T, (8, 1)).astype(np.uint16)


def unstriped(offs):
    return offs[:16].T.reshape(-1).astype(np.int64)


E2M1 = np.array([0.0, 0.5, 1.0, 1.5, 2.0, 3.0, 4.0, 6.0, -0.0, -0.5, -1.0, -1.5, -2.0, -3.0, -4.0, -6.0])


def pack_weight(w, fmt):
    k, n = w.shape
    w = f64(np.asarray(w, np.float32).astype(ml_dtypes.bfloat16)).reshape(k // 32, 32, n)
    amax = np.abs(w).max(1)
    if fmt == "e4m3":
        byte = np.frexp(amax)[1] - 1 + 127 - 7
    else:
        mant, ex = np.frexp(amax / 6.0)
        byte = np.where(mant > 0.5, ex, ex - 1) + 127
    byte = np.clip(np.where(amax > 0, byte, 1), 1, 254)
    scaled = (w * np.exp2(127.0 - byte)[:, None, :]).reshape(k, n).astype(np.float32)
    by_word = np.ascontiguousarray(scaled.reshape(k // 512, 128, 4, n).transpose(0, 1, 3, 2))
    if fmt == "e4m3":
        words = by_word.astype(ml_dtypes.float8_e4m3fn).view(np.uint8)
    else:
        c = by_word.astype(ml_dtypes.float4_e2m1fn).view(np.uint8) & 0xF
        words = (c[..., 0::2] | (c[..., 1::2] << 4)).reshape(k // 512, 128, 2 * n)
    return np.ascontiguousarray(words), np.ascontiguousarray(byte.astype(np.uint8).reshape(k // 512, 16, n))


def unpack_weight(words, scales, fmt):
    g, _, n = scales.shape
    words = np.ascontiguousarray(words).reshape(g, 128, n, -1)
    if fmt == "e4m3":
        vals = words.view(ml_dtypes.float8_e4m3fn).astype(np.float64)
    else:
        nib = np.empty((g, 128, n, 4), np.uint8)
        nib[..., 0::2] = words & 0xF
        nib[..., 1::2] = words >> 4
        vals = E2M1[nib]
    vals = vals * np.repeat(np.exp2(scales.astype(np.float64) - 127.0), 8, axis=1)[..., None]
    return vals.transpose(0, 1, 3, 2).reshape(g * 512, n)


D, T, I, Q, J, U, M = 512, 2048, 512, 128, 512, 1024, 2048


def setup_inputs():
    n = np.random.standard_normal
    idx = np.random.permutation(T)[:I]
    idx2 = np.random.permutation(U)[:J]
    idx3 = np.random.permutation(M)[:I]
    fd = mx_kscale(D)
    fj = mx_kscale(J)
    tiesp = pack_weight(n((J, T)) * 0.08 / fj[:, None], "e2m1")
    return {
        "query": (n((D, Q)) * 1.0 / np.sqrt(D) * fd[:, None]).astype(np.float32),
        "hubs": (n((D, U)) / fd[:, None]).astype(np.float32),
        "hf": (np.random.uniform(0.5, 2.0, (J, 1)) * fj[:, None]).astype(np.float32),
        "ties_words": tiesp[0],
        "ties_scales": tiesp[1],
        "old": (np.random.uniform(0.0, 2.0, (Q, M))).astype(np.float32),
        "fade": (np.random.uniform(0.3, 0.9, (Q, 1))).astype(np.float32),
        "offs": striped(idx),
        "offs2": striped(idx2),
        "offs3": striped(idx3),
    }


def reference(query, hubs, hf, ties_words, ties_scales, old, fade, offs, offs2, offs3):
    idx = unstriped(offs)
    idx2 = unstriped(offs2)
    idx3 = unstriped(offs3)
    tiesu = unpack_weight(ties_words, ties_scales, "e2m1")
    hubsidx2q = mxq(f64(hubs)[:, idx2], 0, "e4m3")
    queryq = mxq(f64(query), 0, "e4m3")
    hb = hubsidx2q.T @ queryq
    hp = np.maximum(hb, 0.0) * f64(hf)
    hpq = mxq(hp, 0, "e4m3")
    tiesidxg = tiesu[:, idx]
    s = hpq.T @ tiesidxg
    p = np.exp(s - np.max(s, axis=1, keepdims=True))
    w = p / np.sum(p, axis=1, keepdims=True)
    ws = w * 256.0
    wf = np.zeros((Q, M))
    wf[:, idx3] = ws
    y = f64(old) * f64(fade) + wf
    return y

@@ -1,0 +1,172 @@
+from contextlib import ExitStack
+
+import concourse.mybir as mybir
+
+D, T, I, Q, J, U, M = 512, 2048, 512, 128, 512, 1024, 2048
+FLOPS = 2 * D * J * Q + 2 * J * Q * I
+
+F32 = mybir.dt.float32
+BF16 = mybir.dt.bfloat16
+I32 = mybir.dt.int32
+U32 = mybir.dt.uint32
+U16 = mybir.dt.uint16
+U8 = mybir.dt.uint8
+FP8X4 = mybir.dt.float8_e4m3fn_x4
+FP4X4 = mybir.dt.float4_e2m1fn_x4
+ALU = mybir.AluOpType
+ACT = mybir.ActivationFunctionType
+
+P = 128
+PACK = 4
+OUT_WIDTHS = (256, 256, 384, 384, 384, 384)
+
+
+def tile_attend_relayed_soft_counts_kernel(tc, query, hubs, hf, ties_words, ties_scales, old, fade, offs, offs2, offs3, out):
+    nc = tc.nc
+    with ExitStack() as ctx:
+        lists = ctx.enter_context(tc.tile_pool(name="lists", bufs=1))
+        sb = ctx.enter_context(tc.tile_pool(name="sb", bufs=1))
+        psum = ctx.enter_context(tc.psum_pool(name="psum", bufs=1))
+
+        tie_list = lists.tile([P, I // 16], U16, name="tie_list")
+        hub_list = lists.tile([P, J // 16], U16, name="hub_list")
+        place_list = lists.tile([P, I // 16], U16, name="place_list")
+
+        scale_pool = sb.tile([P, T], U8, name="scale_pool", tag="scale_pool_then_old")
+        tie_scale = sb.tile([P, I], U8, name="tie_scale", align_bytes=64)
+        window = sb.tile([P, M], F32, name="window")
+        nc.vector.memset(scale_pool[0:112, :].bitcast(I32), 0)
+        nc.vector.memset(tie_scale[:].bitcast(I32), 0)
+        nc.gpsimd.memset(window[:], 0.0)
+
+        hub_rows = hubs.rearrange("(p t) u -> p t u", t=PACK)
+        raw01 = sb.tile([P, 2, U], F32, name="raw01")
+        raw23a = sb.tile([P, 2, U // 2], F32, name="raw23a")
+        raw23b = sb.tile([P, 2, U // 2], F32, name="raw23b")
+        q_raw = sb.tile([P, PACK, Q], F32, name="q_raw")
+        word_pool = sb.tile([P, T], U16, name="word_pool")
+        hf_sb = sb.tile([P, PACK], F32, name="hf_sb")
+        fade_sb = sb.tile([P, 1], F32, name="fade_sb")
+
+        nc.sync.dma_start(tie_list[:], offs)
+        nc.scalar.dma_start(scale_pool[112:128, :].bitcast(I32), ties_scales[0].bitcast(I32))
+        nc.sync.dma_start(raw01[:], hub_rows[:, 0:2, :])
+        nc.sync.dma_start(hub_list[:], offs2)
+        nc.sync.dma_start(raw23a[:], hub_rows[:, 2:4, 0 : U // 2])
+        nc.sync.dma_start(raw23b[:], hub_rows[:, 2:4, U // 2 : U])
+        nc.sync.dma_start(q_raw[:], query.rearrange("(p t) q -> p t q", t=PACK))
+        nc.sync.dma_start(word_pool[:].bitcast(I32), ties_words[0].bitcast(I32))
+        nc.sync.dma_start(hf_sb[:], hf.rearrange("(p r) o -> p (r o)", r=PACK))
+        nc.sync.dma_start(place_list[:], offs3)
+        nc.sync.dma_start(fade_sb[:], fade)
+
+        picked_scale = sb.tile([P, I], U8, name="picked_scale")
+        nc.vector.tensor_copy(picked_scale[:], scale_pool[:].indirect(tie_list[:]))
+        for quad in range(4):
+            nc.sync.dma_start(
+                tie_scale[32 * quad : 32 * quad + 4, :].bitcast(I32),
+                picked_scale[112 + 4 * quad : 112 + 4 * quad + 4, :].bitcast(I32),
+            )
+        old_sb = sb.tile([P, M], F32, name="old_sb", tag="scale_pool_then_old")
+        nc.sync.dma_start(old_sb[:], old)
+
+        pairs = [sb.tile([P, U], F32, name=f"pairs{u}") for u in range(2)]
+
+        def cast(engine, dst, raw, dst_col, lo, hi):
+            o = dst[:, dst_col + lo : dst_col + hi].bitcast(BF16).rearrange("p (c t) -> p c t", t=2)
+            i = raw[:, :, lo:hi].rearrange("p t c -> p c t")
+            if engine == "vector":
+                nc.vector.tensor_copy(o, i)
+            else:
+                nc.scalar.activation(o, i, ACT.Copy)
+
+        picked = sb.tile([P, 2, J], F32, name="picked")
+        cast("vector", pairs[0], raw01, 0, 0, 688)
+        cast("scalar", pairs[0], raw01, 0, 688, U)
+        nc.vector.tensor_copy(picked[:, 0, :], pairs[0][:].indirect(hub_list[:]))
+        cast("scalar", pairs[1], raw23a, 0, 0, U // 2)
+        cast("vector", pairs[1], raw23b, U // 2, 0, 344)
+        cast("scalar", pairs[1], raw23b, U // 2, 344, U // 2)
+        nc.vector.tensor_copy(picked[:, 1, :], pairs[1][:].indirect(hub_list[:]))
+
+        q_bf = sb.tile([P, Q * PACK], BF16, name="q_bf", align_bytes=64)
+        nc.scalar.activation(
+            q_bf[:].rearrange("p (c i t) -> p c t i", i=4, t=PACK),
+            q_raw[:].rearrange("p t (c i) -> p c t i", i=4),
+            ACT.Copy,
+        )
+
+        hub_bf = sb.tile([P, J * PACK], BF16, name="hub_bf", tag="hub_bf_then_tie_words", align_bytes=64)
+        nc.vector.tensor_copy(
+            hub_bf[:].bitcast(F32).rearrange("p (r a b u) -> p a r b u", r=PACK, b=2, u=2),
+            picked[:].rearrange("p u (a b r) -> p a r b u", b=2, r=PACK),
+        )
+        q_codes = sb.tile([P, Q], U32, name="q_codes", align_bytes=64)
+        q_scale = sb.tile([P, Q], U8, name="q_scale", align_bytes=64)
+        nc.vector.quantize_mx(out=q_codes[:].bitcast(FP8X4), scales=q_scale[:], in_=q_bf[:])
+        hub_codes = sb.tile([P, J], U32, name="hub_codes", align_bytes=64)
+        hub_scale = sb.tile([P, J], U8, name="hub_scale", align_bytes=64)
+        nc.vector.quantize_mx(out=hub_codes[:].bitcast(FP8X4), scales=hub_scale[:], in_=hub_bf[:])
+
+        tie_words = sb.tile([P, I], U16, name="tie_words", tag="hub_bf_then_tie_words", align_bytes=64)
+        nc.vector.tensor_copy(tie_words[:], word_pool[:].indirect(tie_list[:]))
+
+        hb = psum.tile([P, PACK, Q], F32, name="hb")
+        for r in range(PACK):
+            cols = slice(r * P, (r + 1) * P)
+            nc.tensor.matmul_mx(
+                out=hb[:, r, :],
+                lhsT=hub_codes[:, cols].bitcast(FP8X4),
+                lhsT_scale=hub_scale[:, cols],
+                rhs=q_codes[:].bitcast(FP8X4),
+                rhs_scale=q_scale[:],
+                start=True,
+                stop=True,
+            )
+        hp_bf = sb.tile([P, Q * PACK], BF16, name="hp_bf", align_bytes=64)
+        nc.vector.scalar_tensor_tensor(
+            out=hp_bf[:].rearrange("p (q r) -> p q r", r=PACK),
+            in0=hb[:].rearrange("p r q -> p q r"),
+            scalar=0.0,
+            in1=hf_sb[:].unsqueeze(1).broadcast_to([P, Q, PACK]),
+            op0=ALU.max,
+            op1=ALU.mult,
+        )
+        hp_codes = sb.tile([P, Q], U32, name="hp_codes", align_bytes=64)
+        hp_scale = sb.tile([P, Q], U8, name="hp_scale", align_bytes=64)
+        nc.vector.quantize_mx(out=hp_codes[:].bitcast(FP8X4), scales=hp_scale[:], in_=hp_bf[:])
+
+        scores = psum.tile([P, I], F32, name="scores")
+        nc.tensor.matmul_mx(
+            out=scores[:],
+            lhsT=hp_codes[:].bitcast(FP8X4),
+            lhsT_scale=hp_scale[:],
+            rhs=tie_words[:].bitcast(FP4X4),
+            rhs_scale=tie_scale[:],
+            start=True,
+            stop=True,
+        )
+
+        neg_max = sb.tile([P, 1], F32, name="neg_max", tag="neg_max_then_faded")
+        nc.vector.tensor_reduce(neg_max[:], scores[:], mybir.AxisListType.X, ALU.max, negate=True)
+        expd = sb.tile([P, I], F32, name="expd")
+        row_sum = sb.tile([P, 1], F32, name="row_sum")
+        nc.scalar.activation(expd[:], scores[:], ACT.Exp, bias=neg_max[:], accum_out=row_sum[:])
+        nc.vector.tensor_copy(window[:].indirect(place_list[:]), expd[:])
+
+        small_sum = sb.tile([P, 1], F32, name="small_sum")
+        nc.scalar.activation(small_sum[:], row_sum[:], ACT.Copy, scale=1.0 / 256.0)
+        row_factor = sb.tile([P, 1], F32, name="row_factor")
+        nc.vector.reciprocal(row_factor[:], small_sum[:])
+
+        faded = sb.tile([P, M], F32, name="faded", tag="neg_max_then_faded")
+        start = 0
+        for n, width in enumerate(OUT_WIDTHS):
+            cols = slice(start, start + width)
+            nc.scalar.activation(faded[:, cols], old_sb[:, cols], ACT.Copy, scale=fade_sb[:])
+            piece = sb.tile([P, width], F32, name=f"piece{n}")
+            nc.vector.scalar_tensor_tensor(
+                out=piece[:], in0=window[:, cols], scalar=row_factor[:], in1=faded[:, cols], op0=ALU.mult, op1=ALU.add
+            )
+            nc.sync.dma_start(out[:, cols], piece[:])
+            start = start + width

@@ -40,9 +40,13 @@ def tile_attend_relayed_soft_counts_kernel(tc, query, hubs, hf, ties_words, ties
         nc.gpsimd.memset(window[:], 0.0)
 
         hub_rows = hubs.rearrange("(p t) u -> p t u", t=PACK)
-        raw01 = sb.tile([P, 2, U], F32, name="raw01")
-        raw23a = sb.tile([P, 2, U // 2], F32, name="raw23a")
-        raw23b = sb.tile([P, 2, U // 2], F32, name="raw23b")
+        pieces = [(0, 0, 1024), (1, 0, 512), (1, 512, 1024)]
+        raws = [sb.tile([P, 2, hi - lo], F32, name=f"raw{n}") for n, (u, lo, hi) in enumerate(pieces)]
+
+        def load(n):
+            u, lo, hi = pieces[n]
+            nc.sync.dma_start(raws[n][:], hub_rows[:, 2 * u : 2 * u + 2, lo:hi])
+
         q_raw = sb.tile([P, PACK, Q], F32, name="q_raw")
         word_pool = sb.tile([P, T], U16, name="word_pool")
         hf_sb = sb.tile([P, PACK], F32, name="hf_sb")
@@ -50,10 +54,10 @@ def tile_attend_relayed_soft_counts_kernel(tc, query, hubs, hf, ties_words, ties
 
         nc.sync.dma_start(tie_list[:], offs)
         nc.scalar.dma_start(scale_pool[112:128, :].bitcast(I32), ties_scales[0].bitcast(I32))
-        nc.sync.dma_start(raw01[:], hub_rows[:, 0:2, :])
+        load(0)
         nc.sync.dma_start(hub_list[:], offs2)
-        nc.sync.dma_start(raw23a[:], hub_rows[:, 2:4, 0 : U // 2])
-        nc.sync.dma_start(raw23b[:], hub_rows[:, 2:4, U // 2 : U])
+        for n in range(1, 3):
+            load(n)
         nc.sync.dma_start(q_raw[:], query.rearrange("(p t) q -> p t q", t=PACK))
         nc.sync.dma_start(word_pool[:].bitcast(I32), ties_words[0].bitcast(I32))
         nc.sync.dma_start(hf_sb[:], hf.rearrange("(p r) o -> p (r o)", r=PACK))
@@ -72,22 +76,29 @@ def tile_attend_relayed_soft_counts_kernel(tc, query, hubs, hf, ties_words, ties
 
         pairs = [sb.tile([P, U], F32, name=f"pairs{u}") for u in range(2)]
 
-        def cast(engine, dst, raw, dst_col, lo, hi):
-            o = dst[:, dst_col + lo : dst_col + hi].bitcast(BF16).rearrange("p (c t) -> p c t", t=2)
-            i = raw[:, :, lo:hi].rearrange("p t c -> p c t")
+        def cast(engine, n, lo, hi):
+            u, first, last = pieces[n]
+            o = pairs[u][:, first + lo : first + hi].bitcast(BF16).rearrange("p (c t) -> p c t", t=2)
+            i = raws[n][:, :, lo:hi].rearrange("p t c -> p c t")
             if engine == "vector":
                 nc.vector.tensor_copy(o, i)
             else:
                 nc.scalar.activation(o, i, ACT.Copy)
 
-        picked = sb.tile([P, 2, J], F32, name="picked")
-        cast("vector", pairs[0], raw01, 0, 0, 688)
-        cast("scalar", pairs[0], raw01, 0, 688, U)
-        nc.vector.tensor_copy(picked[:, 0, :], pairs[0][:].indirect(hub_list[:]))
-        cast("scalar", pairs[1], raw23a, 0, 0, U // 2)
-        cast("vector", pairs[1], raw23b, U // 2, 0, 344)
-        cast("scalar", pairs[1], raw23b, U // 2, 344, U // 2)
-        nc.vector.tensor_copy(picked[:, 1, :], pairs[1][:].indirect(hub_list[:]))
+        parts = [(0, 320), (320, 512)]
+        picked = [sb.tile([P, 2, hi - lo], F32, name=f"picked{h}") for h, (lo, hi) in enumerate(parts)]
+
+        def gather(u):
+            for h, (lo, hi) in enumerate(parts):
+                nc.vector.tensor_copy(picked[h][:, u, :], pairs[u][:].indirect(hub_list[:, lo // 16 : hi // 16]))
+
+        cast("vector", 0, 0, 688)
+        cast("scalar", 0, 688, 1024)
+        gather(0)
+        cast("scalar", 1, 0, 512)
+        cast("vector", 2, 0, 320)
+        cast("scalar", 2, 320, 512)
+        gather(1)
 
         q_bf = sb.tile([P, Q * PACK], BF16, name="q_bf", align_bytes=64)
         nc.scalar.activation(
@@ -97,10 +108,10 @@ def tile_attend_relayed_soft_counts_kernel(tc, query, hubs, hf, ties_words, ties
         )
 
         hub_bf = sb.tile([P, J * PACK], BF16, name="hub_bf", tag="hub_bf_then_tie_words", align_bytes=64)
-        nc.vector.tensor_copy(
-            hub_bf[:].bitcast(F32).rearrange("p (r a b u) -> p a r b u", r=PACK, b=2, u=2),
-            picked[:].rearrange("p u (a b r) -> p a r b u", b=2, r=PACK),
-        )
+        dealt = hub_bf[:].bitcast(F32).rearrange("p (r a b u) -> p a r b u", r=PACK, b=2, u=2)
+        for h, (lo, hi) in enumerate(parts):
+            copy = nc.vector.tensor_copy if h == 1 else nc.scalar.copy
+            copy(dealt[:, lo // 8 : hi // 8], picked[h][:].rearrange("p u (a b r) -> p a r b u", b=2, r=PACK))
         q_codes = sb.tile([P, Q], U32, name="q_codes", align_bytes=64)
         q_scale = sb.tile([P, Q], U8, name="q_scale", align_bytes=64)
         nc.vector.quantize_mx(out=q_codes[:].bitcast(FP8X4), scales=q_scale[:], in_=q_bf[:])

@@ -37,7 +37,7 @@ def tile_attend_relayed_soft_counts_kernel(tc, query, hubs, hf, ties_words, ties
         window = sb.tile([P, M], F32, name="window")
         nc.vector.memset(scale_pool[0:112, :].bitcast(I32), 0)
         nc.vector.memset(tie_scale[:].bitcast(I32), 0)
-        nc.gpsimd.memset(window[:], 0.0)
+        nc.vector.memset(window[:], 0.0)
 
         hub_rows = hubs.rearrange("(p t) u -> p t u", t=PACK)
         pieces = [(0, 0, 1024), (1, 0, 512), (1, 512, 1024)]

from contextlib import ExitStack

import concourse.mybir as mybir

D, T, I, Q, J, U, M = 512, 2048, 512, 128, 512, 1024, 2048
FLOPS = 2 * D * J * Q + 2 * J * Q * I

F32 = mybir.dt.float32
BF16 = mybir.dt.bfloat16
I32 = mybir.dt.int32
U32 = mybir.dt.uint32
U16 = mybir.dt.uint16
U8 = mybir.dt.uint8
FP8X4 = mybir.dt.float8_e4m3fn_x4
FP4X4 = mybir.dt.float4_e2m1fn_x4
ALU = mybir.AluOpType
ACT = mybir.ActivationFunctionType

P = 128
PACK = 4
OUT_WIDTHS = (256, 256, 384, 384, 384, 384)


def tile_attend_relayed_soft_counts_kernel(tc, query, hubs, hf, ties_words, ties_scales, old, fade, offs, offs2, offs3, out):
    nc = tc.nc
    with ExitStack() as ctx:
        lists = ctx.enter_context(tc.tile_pool(name="lists", bufs=1))
        sb = ctx.enter_context(tc.tile_pool(name="sb", bufs=1))
        psum = ctx.enter_context(tc.psum_pool(name="psum", bufs=1))

        tie_list = lists.tile([P, I // 16], U16, name="tie_list")
        hub_list = lists.tile([P, J // 16], U16, name="hub_list")
        place_list = lists.tile([P, I // 16], U16, name="place_list")

        scale_pool = sb.tile([P, T], U8, name="scale_pool", tag="scale_pool_then_old")
        tie_scale = sb.tile([P, I], U8, name="tie_scale", align_bytes=64)
        window = sb.tile([P, M], F32, name="window")
        nc.vector.memset(scale_pool[0:112, :].bitcast(I32), 0)
        nc.vector.memset(tie_scale[:].bitcast(I32), 0)
        nc.vector.memset(window[:], 0.0)

        hub_rows = hubs.rearrange("(p t) u -> p t u", t=PACK)
        pieces = [(0, 0, 1024), (1, 0, 512), (1, 512, 1024)]
        raws = [sb.tile([P, 2, hi - lo], F32, name=f"raw{n}") for n, (u, lo, hi) in enumerate(pieces)]

        def load(n):
            u, lo, hi = pieces[n]
            nc.sync.dma_start(raws[n][:], hub_rows[:, 2 * u : 2 * u + 2, lo:hi])

        q_raw = sb.tile([P, PACK, Q], F32, name="q_raw")
        word_pool = sb.tile([P, T], U16, name="word_pool")
        hf_sb = sb.tile([P, PACK], F32, name="hf_sb")
        fade_sb = sb.tile([P, 1], F32, name="fade_sb")

        nc.sync.dma_start(tie_list[:], offs)
        nc.scalar.dma_start(scale_pool[112:128, :].bitcast(I32), ties_scales[0].bitcast(I32))
        load(0)
        nc.sync.dma_start(hub_list[:], offs2)
        for n in range(1, 3):
            load(n)
        nc.sync.dma_start(q_raw[:], query.rearrange("(p t) q -> p t q", t=PACK))
        nc.sync.dma_start(word_pool[:].bitcast(I32), ties_words[0].bitcast(I32))
        nc.sync.dma_start(hf_sb[:], hf.rearrange("(p r) o -> p (r o)", r=PACK))
        nc.sync.dma_start(place_list[:], offs3)
        nc.sync.dma_start(fade_sb[:], fade)

        picked_scale = sb.tile([P, I], U8, name="picked_scale")
        nc.vector.tensor_copy(picked_scale[:], scale_pool[:].indirect(tie_list[:]))
        for quad in range(4):
            nc.sync.dma_start(
                tie_scale[32 * quad : 32 * quad + 4, :].bitcast(I32),
                picked_scale[112 + 4 * quad : 112 + 4 * quad + 4, :].bitcast(I32),
            )
        old_sb = sb.tile([P, M], F32, name="old_sb", tag="scale_pool_then_old")
        nc.sync.dma_start(old_sb[:], old)

        pairs = [sb.tile([P, U], F32, name=f"pairs{u}") for u in range(2)]

        def cast(engine, n, lo, hi):
            u, first, last = pieces[n]
            o = pairs[u][:, first + lo : first + hi].bitcast(BF16).rearrange("p (c t) -> p c t", t=2)
            i = raws[n][:, :, lo:hi].rearrange("p t c -> p c t")
            if engine == "vector":
                nc.vector.tensor_copy(o, i)
            else:
                nc.scalar.activation(o, i, ACT.Copy)

        parts = [(0, 320), (320, 512)]
        picked = [sb.tile([P, 2, hi - lo], F32, name=f"picked{h}") for h, (lo, hi) in enumerate(parts)]

        def gather(u):
            for h, (lo, hi) in enumerate(parts):
                nc.vector.tensor_copy(picked[h][:, u, :], pairs[u][:].indirect(hub_list[:, lo // 16 : hi // 16]))

        cast("vector", 0, 0, 688)
        cast("scalar", 0, 688, 1024)
        gather(0)
        cast("scalar", 1, 0, 512)
        cast("vector", 2, 0, 320)
        cast("scalar", 2, 320, 512)
        gather(1)

        q_bf = sb.tile([P, Q * PACK], BF16, name="q_bf", align_bytes=64)
        nc.scalar.activation(
            q_bf[:].rearrange("p (c i t) -> p c t i", i=4, t=PACK),
            q_raw[:].rearrange("p t (c i) -> p c t i", i=4),
            ACT.Copy,
        )

        hub_bf = sb.tile([P, J * PACK], BF16, name="hub_bf", tag="hub_bf_then_tie_words", align_bytes=64)
        dealt = hub_bf[:].bitcast(F32).rearrange("p (r a b u) -> p a r b u", r=PACK, b=2, u=2)
        for h, (lo, hi) in enumerate(parts):
            copy = nc.vector.tensor_copy if h == 1 else nc.scalar.copy
            copy(dealt[:, lo // 8 : hi // 8], picked[h][:].rearrange("p u (a b r) -> p a r b u", b=2, r=PACK))
        q_codes = sb.tile([P, Q], U32, name="q_codes", align_bytes=64)
        q_scale = sb.tile([P, Q], U8, name="q_scale", align_bytes=64)
        nc.vector.quantize_mx(out=q_codes[:].bitcast(FP8X4), scales=q_scale[:], in_=q_bf[:])
        hub_codes = sb.tile([P, J], U32, name="hub_codes", align_bytes=64)
        hub_scale = sb.tile([P, J], U8, name="hub_scale", align_bytes=64)
        nc.vector.quantize_mx(out=hub_codes[:].bitcast(FP8X4), scales=hub_scale[:], in_=hub_bf[:])

        tie_words = sb.tile([P, I], U16, name="tie_words", tag="hub_bf_then_tie_words", align_bytes=64)
        nc.vector.tensor_copy(tie_words[:], word_pool[:].indirect(tie_list[:]))

        hb = psum.tile([P, PACK, Q], F32, name="hb")
        for r in range(PACK):
            cols = slice(r * P, (r + 1) * P)
            nc.tensor.matmul_mx(
                out=hb[:, r, :],
                lhsT=hub_codes[:, cols].bitcast(FP8X4),
                lhsT_scale=hub_scale[:, cols],
                rhs=q_codes[:].bitcast(FP8X4),
                rhs_scale=q_scale[:],
                start=True,
                stop=True,
            )
        hp_bf = sb.tile([P, Q * PACK], BF16, name="hp_bf", align_bytes=64)
        nc.vector.scalar_tensor_tensor(
            out=hp_bf[:].rearrange("p (q r) -> p q r", r=PACK),
            in0=hb[:].rearrange("p r q -> p q r"),
            scalar=0.0,
            in1=hf_sb[:].unsqueeze(1).broadcast_to([P, Q, PACK]),
            op0=ALU.max,
            op1=ALU.mult,
        )
        hp_codes = sb.tile([P, Q], U32, name="hp_codes", align_bytes=64)
        hp_scale = sb.tile([P, Q], U8, name="hp_scale", align_bytes=64)
        nc.vector.quantize_mx(out=hp_codes[:].bitcast(FP8X4), scales=hp_scale[:], in_=hp_bf[:])

        scores = psum.tile([P, I], F32, name="scores")
        nc.tensor.matmul_mx(
            out=scores[:],
            lhsT=hp_codes[:].bitcast(FP8X4),
            lhsT_scale=hp_scale[:],
            rhs=tie_words[:].bitcast(FP4X4),
            rhs_scale=tie_scale[:],
            start=True,
            stop=True,
        )

        neg_max = sb.tile([P, 1], F32, name="neg_max", tag="neg_max_then_faded")
        nc.vector.tensor_reduce(neg_max[:], scores[:], mybir.AxisListType.X, ALU.max, negate=True)
        expd = sb.tile([P, I], F32, name="expd")
        row_sum = sb.tile([P, 1], F32, name="row_sum")
        nc.scalar.activation(expd[:], scores[:], ACT.Exp, bias=neg_max[:], accum_out=row_sum[:])
        nc.vector.tensor_copy(window[:].indirect(place_list[:]), expd[:])

        small_sum = sb.tile([P, 1], F32, name="small_sum")
        nc.scalar.activation(small_sum[:], row_sum[:], ACT.Copy, scale=1.0 / 256.0)
        row_factor = sb.tile([P, 1], F32, name="row_factor")
        nc.vector.reciprocal(row_factor[:], small_sum[:])

        faded = sb.tile([P, M], F32, name="faded", tag="neg_max_then_faded")
        start = 0
        for n, width in enumerate(OUT_WIDTHS):
            cols = slice(start, start + width)
            nc.scalar.activation(faded[:, cols], old_sb[:, cols], ACT.Copy, scale=fade_sb[:])
            piece = sb.tile([P, width], F32, name=f"piece{n}")
            nc.vector.scalar_tensor_tensor(
                out=piece[:], in0=window[:, cols], scalar=row_factor[:], in1=faded[:, cols], op0=ALU.mult, op1=ALU.add
            )
            nc.sync.dma_start(out[:, cols], piece[:])
            start = start + width
